import numpy as np
import ml_dtypes


def mxq(x, axis, fmt="e4m3"):
    dtype, down = {"e4m3": (ml_dtypes.float8_e4m3fn, 7), "e5m2": (ml_dtypes.float8_e5m2, 14)}[fmt]
    v = np.moveaxis(np.asarray(x, np.float32).astype(ml_dtypes.bfloat16).astype(np.float64), axis, -1)
    blocks = v.reshape(v.shape[:-1] + (-1, 32))
    amax = np.abs(blocks).max(-1, keepdims=True)
    byte = np.maximum(np.where(amax > 0, np.frexp(amax)[1] - 1 + 127, 0) - down, 1)
    scale = np.exp2(byte - 127.0)
    codes = (blocks / scale).astype(np.float32).astype(dtype).astype(np.float64)
    return np.moveaxis((codes * scale).reshape(v.shape), -1, axis)


WIDE = False


def mx_kscale(k):
    if not WIDE:
        return np.ones(k)
    levels = np.array([10, -10, 5, -5, 0])
    if k % 512:
        return np.exp2(np.random.permutation(np.resize(levels, k // 32))).repeat(32)
    a = np.empty((k // 512, 16))
    for p in range(k // 512):
        a[p, :8] = np.random.permutation(np.resize(levels, 8))
        for g in range(8):
            far = levels[np.abs(levels - a[p, g]) >= 10]
            a[p, g + 8] = far[np.random.randint(len(far))]
    return np.exp2(a.ravel()).repeat(32)


def f64(x):
    return np.asarray(x).astype(np.float64)


def striped(idx):
    return np.tile(idx.reshape(-1, 16).T, (8, 1)).astype(np.uint16)


def unstriped(offs):
    return offs[:16].T.reshape(-1).astype(np.int64)


def pack_weight(w):
    k, n = w.shape
    w = f64(np.asarray(w, np.float32).astype(ml_dtypes.bfloat16)).reshape(k // 32, 32, n)
    amax = np.abs(w).max(1)
    byte = np.clip(np.where(amax > 0, np.frexp(amax)[1] - 1 + 127 - 7, 1), 1, 254)
    scaled = (w * np.exp2(127.0 - byte)[:, None, :]).reshape(k, n).astype(np.float32)
    words = np.ascontiguousarray(scaled.reshape(k // 512, 128, 4, n).transpose(0, 1, 3, 2)).astype(ml_dtypes.float8_e4m3fn).view(np.uint8)
    return words, np.ascontiguousarray(byte.astype(np.uint8).reshape(k // 512, 16, n))


def unpack_weight(words, scales):
    g, p, n, _ = words.shape
    vals = np.ascontiguousarray(words).view(ml_dtypes.float8_e4m3fn).astype(np.float64) * np.repeat(np.exp2(scales.astype(np.float64) - 127.0), 8, axis=1)[..., None]
    return vals.transpose(0, 1, 3, 2).reshape(g * 512, n)


def relu(v):
    return np.maximum(v, 0.0)


K, T, E, C, N = 2048, 1024, 8, 256, 128


def by_expert(wq, xq):
    return np.concatenate([wq[e].T @ xq[:, e * C:(e + 1) * C] for e in range(E)], axis=1)


def setup_inputs():
    n = np.random.standard_normal
    s = mx_kscale(K)[:, None]
    first = np.random.permutation(np.repeat(np.arange(E), T // E))
    second = (first + 1 + np.random.permutation(np.repeat(np.arange(E - 1), -(-T // (E - 1)))[:T])) % E
    while np.bincount(second, minlength=E).max() != T // E:
        load = np.bincount(second, minlength=E); hi, lo = int(load.argmax()), int(load.argmin())
        t = np.flatnonzero((second == hi) & (first != lo))[0]; second[t] = lo
    slot_token = np.empty(E * C, np.int64); pos = np.empty((2, T), np.int64); fill = np.zeros(E, np.int64)
    place = np.stack([np.random.permutation(C) for _ in range(E)])
    for r, deal in enumerate((first, second)):
        for t in np.random.permutation(T):
            e = deal[t]; j = e * C + place[e, fill[e]]; fill[e] += 1; slot_token[j] = t; pos[r, t] = j
    g = np.random.uniform(0.2, 0.8, T)
    packed = [pack_weight(m) for m in n((E, K, N)) / np.sqrt(K) / s[None]]
    return {
        "xT": (n((K, T)) * s).astype(np.float32),
        "w_words": np.stack([m[0] for m in packed]),
        "w_scales": np.stack([m[1] for m in packed]),
        "b": (0.3 * n((N, E))).astype(np.float32),
        "gate": np.stack([np.tile(g, (N, 1)), np.tile(1.0 - g, (N, 1))]).astype(np.float32),
        "offs": striped(slot_token),
        "pos1": striped(pos[0]),
        "pos2": striped(pos[1]),
    }


def reference(xT, w_words, w_scales, b, gate, offs, pos1, pos2):
    idx = unstriped(offs)
    xq = mxq(f64(xT)[:, idx], 0, "e4m3")
    w = np.stack([unpack_weight(w_words[e], w_scales[e]) for e in range(E)])
    y = by_expert(w, xq)
    y = relu(y + np.repeat(f64(b), C, axis=1))
    return f64(gate[0]) * y[:, unstriped(pos1)] + f64(gate[1]) * y[:, unstriped(pos2)]

@@ -1,0 +1,151 @@
+from contextlib import ExitStack
+
+import concourse.mybir as mybir
+
+K, T, E, C, N = 2048, 1024, 8, 256, 128
+P = 128
+PACK = 4
+PASSES = K // (P * PACK)
+S = E * C
+
+F32 = mybir.dt.float32
+BF16 = mybir.dt.bfloat16
+U32 = mybir.dt.uint32
+I32 = mybir.dt.int32
+U16 = mybir.dt.uint16
+U8 = mybir.dt.uint8
+FP8X4 = mybir.dt.float8_e4m3fn_x4
+RELU = mybir.ActivationFunctionType.Relu
+MULT = mybir.AluOpType.mult
+ADD = mybir.AluOpType.add
+MAX = mybir.AluOpType.max
+
+FLOPS = 2 * S * K * N
+
+XCHUNKS = [[(0, 256), (256, 512), (512, 768), (768, 896), (896, 1024)]] + [[(0, 512), (512, 1024)]] * 3
+GCHUNKS = [(0, 768), (768, 1536), (1536, 2048)]
+WIDE = [(0, 1024), (1024, 2048)]
+BCHUNKS = [(0, 512), (512, 1280), (1280, 2048)]
+OCHUNKS = [(0, 512), (512, 768), (768, 1024)]
+
+
+def tile_routed_moe_kernel(tc, xT, w_words, w_scales, b, gate, offs, pos1, pos2, out):
+    nc = tc.nc
+    with ExitStack() as ctx:
+        keep = ctx.enter_context(tc.tile_pool(name="keep", bufs=1))
+        psum = ctx.enter_context(tc.psum_pool(name="psum", bufs=1))
+
+        offs_t = keep.tile([P, S // 16], U16, name="offs_t")
+        pos1_t = keep.tile([P, T // 16], U16, name="pos1_t")
+        pos2_t = keep.tile([P, T // 16], U16, name="pos2_t")
+        tok_scales = keep.tile([P, T], U8, name="tok_scales", align_bytes=64)
+        tok_words = [keep.tile([P, 2 * T if a < PASSES - 1 else T], I32, name=f"tok_words{a}", align_bytes=64) for a in range(PASSES)]
+        slot_words = [keep.tile([P, S], U32, name=f"slot_words{a}", align_bytes=64) for a in range(PASSES)]
+        slot_scales = keep.tile([P, S], U8, name="slot_scales", align_bytes=64)
+        w_t = keep.tile([P, E, PASSES, N], U32, name="w_t", align_bytes=64)
+        ws_t = keep.tile([P, E * PASSES, N], U8, name="ws_t", align_bytes=64)
+        b_t = keep.tile([P, E], F32, name="b_t")
+        gate_t = keep.tile([P, 2, T], F32, name="gate_t")
+        y = keep.tile([P, S], F32, name="y")
+        first = keep.tile([P, T], F32, name="first")
+        second = keep.tile([P, T], F32, name="second")
+        warm = keep.tile([P, 1], F32, name="warm")
+
+        nc.gpsimd.memset(tok_scales[:], 0)
+        nc.vector.memset(ws_t[:].rearrange("p g n -> p (g n)").bitcast(I32), 0)
+        nc.vector.memset(warm[:], 0.0)
+        nc.scalar.activation(warm[:], warm[:], RELU)
+        for a in range(PASSES - 1):
+            nc.vector.memset(tok_words[a][:, T:], 0)
+
+        xv = xT.rearrange("(a p t) n -> a p t n", p=P, t=PACK)
+        raws = {}
+        for a in range(PASSES):
+            for lo, hi in XCHUNKS[a]:
+                raw = keep.tile([P, PACK, hi - lo], F32, name=f"raw{a}_{lo}")
+                nc.sync.dma_start(out=raw[:], in_=xv[a, :, :, lo:hi])
+                raws[a, lo] = raw
+                if a == 0 and lo == 0:
+                    nc.sync.dma_start(offs_t[:], offs)
+        for q in range(4):
+            nc.sync.dma_start(
+                out=ws_t[32 * q : 32 * q + 4, :, :].rearrange("r g n -> r (g n)").bitcast(I32).rearrange("r (g n) -> r g n", g=E * PASSES),
+                in_=w_scales.bitcast(I32).rearrange("e a r n -> r (e a) n")[4 * q : 4 * q + 4],
+            )
+        wv = w_words.rearrange("e a p n r -> p (e a) (n r)").bitcast(I32)
+        wt = w_t[:].rearrange("p e a n -> p (e a) n").bitcast(I32)
+        half = E * PASSES // 2
+        for h in range(2):
+            nc.sync.dma_start(out=wt[:, h * half : (h + 1) * half, :], in_=wv[:, h * half : (h + 1) * half, :])
+        nc.sync.dma_start(b_t[:], b)
+        nc.sync.dma_start(pos1_t[:], pos1)
+        nc.sync.dma_start(pos2_t[:], pos2)
+        for r in range(2):
+            nc.sync.dma_start(gate_t[:, r, :], gate[r])
+
+        def quantise(a):
+            for i, (lo, hi) in enumerate(XCHUNKS[a]):
+                w = hi - lo
+                grouped = keep.tile([P, w * PACK], BF16, name=f"grouped{a}_{lo}", align_bytes=64)
+                dst = grouped[:].rearrange("p (c i t) -> p c t i", i=4, t=PACK)
+                src = raws[a, lo][:].rearrange("p t (c i) -> p c t i", i=4)
+                if a == 0 and i % 2 == 1:
+                    nc.vector.tensor_copy(dst, src)
+                else:
+                    nc.scalar.copy(dst, src)
+                nc.vector.quantize_mx(
+                    out=tok_words[a][:, lo:hi].bitcast(FP8X4),
+                    scales=tok_scales[4 * a : P, lo:hi],
+                    in_=grouped[:],
+                )
+
+        def gather_words(a, lo, hi):
+            nc.vector.tensor_copy(slot_words[a][:, lo:hi], tok_words[a][:].bitcast(U32).indirect(offs_t[:, lo // 16 : hi // 16]))
+
+        ps = [psum.tile([P, C], F32, name=f"ps{e}") for e in range(E)]
+
+        def multiply(a, e):
+            nc.tensor.matmul_mx(
+                out=ps[e][:],
+                lhsT=w_t[:, e, a, :].bitcast(FP8X4),
+                lhsT_scale=ws_t[:, e * PASSES + a, :],
+                rhs=slot_words[a][:, e * C : (e + 1) * C].bitcast(FP8X4),
+                rhs_scale=slot_scales[4 * a : P, e * C : (e + 1) * C],
+                start=(a == 0),
+                stop=(a == PASSES - 1),
+            )
+
+        for a in range(PASSES):
+            quantise(a)
+            if a < PASSES - 1:
+                for lo, hi in WIDE:
+                    gather_words(a, lo, hi)
+        for lo, hi in BCHUNKS:
+            nc.vector.tensor_copy(slot_scales[:, lo:hi], tok_scales[:].indirect(offs_t[:, lo // 16 : hi // 16]))
+            for a in range(PASSES - 1):
+                for e in range(lo // C, hi // C):
+                    multiply(a, e)
+        for lo, hi in GCHUNKS:
+            gather_words(PASSES - 1, lo, hi)
+            for e in range(lo // C, hi // C):
+                multiply(PASSES - 1, e)
+                cols = slice(e * C, (e + 1) * C)
+                if e == E - 1:
+                    nc.vector.tensor_scalar(y[:, cols], ps[e][:], b_t[:, e : e + 1], 0.0, ADD, MAX)
+                else:
+                    nc.scalar.activation(y[:, cols], ps[e][:], RELU, bias=b_t[:, e : e + 1])
+
+        nc.vector.tensor_tensor(first[:], y[:].indirect(pos1_t[:]), gate_t[:, 0, :], MULT)
+        pend = []
+        for lo, hi in OCHUNKS:
+            nc.vector.tensor_tensor(second[:, lo:hi], y[:].indirect(pos2_t[:, lo // 16 : hi // 16]), gate_t[:, 1, lo:hi], MULT)
+            pend.append((lo, hi))
+            if len(pend) > 1:
+                combine(nc, keep, first, second, out, *pend.pop(0))
+        combine(nc, keep, first, second, out, *pend.pop(0))
+
+
+def combine(nc, keep, first, second, out, lo, hi):
+    res = keep.tile([P, hi - lo], F32, name=f"res{lo}")
+    nc.vector.tensor_tensor(res[:], first[:, lo:hi], second[:, lo:hi], ADD)
+    nc.sync.dma_start(out[:, lo:hi], res[:])

@@ -22,8 +22,14 @@ MAX = mybir.AluOpType.max
 
 FLOPS = 2 * S * K * N
 
-XCHUNKS = [[(0, 256), (256, 512), (512, 768), (768, 896), (896, 1024)]] + [[(0, 512), (512, 1024)]] * 3
-GCHUNKS = [(0, 768), (768, 1536), (1536, 2048)]
+XCHUNKS = [
+    [(0, 512), (512, 768), (768, 1024)],
+    [(0, 256), (256, 512), (512, 768), (768, 1024)],
+    [(0, 512), (512, 1024)],
+    [(0, 512), (512, 1024)],
+]
+QCHUNKS = [XCHUNKS[0], XCHUNKS[2], XCHUNKS[2], XCHUNKS[2]]
+GCHUNKS = [(0, 1024), (1024, 1792), (1792, 2048)]
 WIDE = [(0, 1024), (1024, 2048)]
 BCHUNKS = [(0, 512), (512, 1280), (1280, 2048)]
 OCHUNKS = [(0, 512), (512, 768), (768, 1024)]
@@ -39,7 +45,7 @@ def tile_routed_moe_kernel(tc, xT, w_words, w_scales, b, gate, offs, pos1, pos2,
         pos1_t = keep.tile([P, T // 16], U16, name="pos1_t")
         pos2_t = keep.tile([P, T // 16], U16, name="pos2_t")
         tok_scales = keep.tile([P, T], U8, name="tok_scales", align_bytes=64)
-        tok_words = [keep.tile([P, 2 * T if a < PASSES - 1 else T], I32, name=f"tok_words{a}", align_bytes=64) for a in range(PASSES)]
+        tok_words = [keep.tile([P, 2 * T], I32, name=f"tok_words{a}", align_bytes=64) for a in range(PASSES)]
         slot_words = [keep.tile([P, S], U32, name=f"slot_words{a}", align_bytes=64) for a in range(PASSES)]
         slot_scales = keep.tile([P, S], U8, name="slot_scales", align_bytes=64)
         w_t = keep.tile([P, E, PASSES, N], U32, name="w_t", align_bytes=64)
@@ -52,10 +58,10 @@ def tile_routed_moe_kernel(tc, xT, w_words, w_scales, b, gate, offs, pos1, pos2,
         warm = keep.tile([P, 1], F32, name="warm")
 
         nc.gpsimd.memset(tok_scales[:], 0)
-        nc.vector.memset(ws_t[:].rearrange("p g n -> p (g n)").bitcast(I32), 0)
+        nc.gpsimd.memset(ws_t[:].rearrange("p g n -> p (g n)").bitcast(I32), 0)
         nc.vector.memset(warm[:], 0.0)
         nc.scalar.activation(warm[:], warm[:], RELU)
-        for a in range(PASSES - 1):
+        for a in range(PASSES):
             nc.vector.memset(tok_words[a][:, T:], 0)
 
         xv = xT.rearrange("(a p t) n -> a p t n", p=P, t=PACK)
@@ -83,20 +89,25 @@ def tile_routed_moe_kernel(tc, xT, w_words, w_scales, b, gate, offs, pos1, pos2,
         for r in range(2):
             nc.sync.dma_start(gate_t[:, r, :], gate[r])
 
+        def cast(engine, grouped, raw, lo, at, w):
+            dst = grouped[:, (lo + at) * PACK : (lo + at + w) * PACK].rearrange("p (c i t) -> p c t i", i=4, t=PACK)
+            engine(dst, raw[:, :, at : at + w].rearrange("p t (c i) -> p c t i", i=4))
+
         def quantise(a):
-            for i, (lo, hi) in enumerate(XCHUNKS[a]):
-                w = hi - lo
-                grouped = keep.tile([P, w * PACK], BF16, name=f"grouped{a}_{lo}", align_bytes=64)
-                dst = grouped[:].rearrange("p (c i t) -> p c t i", i=4, t=PACK)
-                src = raws[a, lo][:].rearrange("p t (c i) -> p c t i", i=4)
-                if a == 0 and i % 2 == 1:
-                    nc.vector.tensor_copy(dst, src)
-                else:
-                    nc.scalar.copy(dst, src)
+            grouped = keep.tile([P, T * PACK], BF16, name=f"grouped{a}", align_bytes=64)
+            for lo, hi in QCHUNKS[a]:
+                for x0, x1 in XCHUNKS[a]:
+                    if lo <= x0 < hi:
+                        w = x1 - x0
+                        if a == 0:
+                            cast(nc.scalar.copy, grouped, raws[a, x0], x0, 0, w // 2)
+                            cast(nc.vector.tensor_copy, grouped, raws[a, x0], x0, w // 2, w // 2)
+                        else:
+                            cast(nc.scalar.copy, grouped, raws[a, x0], x0, 0, w)
                 nc.vector.quantize_mx(
                     out=tok_words[a][:, lo:hi].bitcast(FP8X4),
                     scales=tok_scales[4 * a : P, lo:hi],
-                    in_=grouped[:],
+                    in_=grouped[:, lo * PACK : hi * PACK],
                 )
 
         def gather_words(a, lo, hi):

@@ -23,16 +23,18 @@ MAX = mybir.AluOpType.max
 FLOPS = 2 * S * K * N
 
 XCHUNKS = [
-    [(0, 512), (512, 768), (768, 1024)],
-    [(0, 256), (256, 512), (512, 768), (768, 1024)],
+    [(0, 512), (512, 896), (896, 1024)],
+    [(0, 384), (384, 768), (768, 1024)],
     [(0, 512), (512, 1024)],
     [(0, 512), (512, 1024)],
 ]
-QCHUNKS = [XCHUNKS[0], XCHUNKS[2], XCHUNKS[2], XCHUNKS[2]]
+QCHUNKS = [[(0, 512), (512, 768), (768, 896), (896, 1024)], XCHUNKS[2], XCHUNKS[2], XCHUNKS[2]]
+SCALAR_SHARE = {512: 192, 384: 144, 128: 48}
 GCHUNKS = [(0, 1024), (1024, 1792), (1792, 2048)]
 WIDE = [(0, 1024), (1024, 2048)]
 BCHUNKS = [(0, 512), (512, 1280), (1280, 2048)]
-OCHUNKS = [(0, 512), (512, 768), (768, 1024)]
+OCHUNKS = [(0, 512), (512, 896), (896, 1024)]
+UNITS = [(e, e * C, (e + 1) * C) for e in range(E)]
 
 
 def tile_routed_moe_kernel(tc, xT, w_words, w_scales, b, gate, offs, pos1, pos2, out):
@@ -71,8 +73,8 @@ def tile_routed_moe_kernel(tc, xT, w_words, w_scales, b, gate, offs, pos1, pos2,
                 raw = keep.tile([P, PACK, hi - lo], F32, name=f"raw{a}_{lo}")
                 nc.sync.dma_start(out=raw[:], in_=xv[a, :, :, lo:hi])
                 raws[a, lo] = raw
-                if a == 0 and lo == 0:
-                    nc.sync.dma_start(offs_t[:], offs)
+            if a == 0:
+                nc.sync.dma_start(offs_t[:], offs)
         for q in range(4):
             nc.sync.dma_start(
                 out=ws_t[32 * q : 32 * q + 4, :, :].rearrange("r g n -> r (g n)").bitcast(I32).rearrange("r (g n) -> r g n", g=E * PASSES),
@@ -80,8 +82,8 @@ def tile_routed_moe_kernel(tc, xT, w_words, w_scales, b, gate, offs, pos1, pos2,
             )
         wv = w_words.rearrange("e a p n r -> p (e a) (n r)").bitcast(I32)
         wt = w_t[:].rearrange("p e a n -> p (e a) n").bitcast(I32)
-        half = E * PASSES // 2
-        for h in range(2):
+        half = E * PASSES // 4
+        for h in range(4):
             nc.sync.dma_start(out=wt[:, h * half : (h + 1) * half, :], in_=wv[:, h * half : (h + 1) * half, :])
         nc.sync.dma_start(b_t[:], b)
         nc.sync.dma_start(pos1_t[:], pos1)
@@ -93,38 +95,55 @@ def tile_routed_moe_kernel(tc, xT, w_words, w_scales, b, gate, offs, pos1, pos2,
             dst = grouped[:, (lo + at) * PACK : (lo + at + w) * PACK].rearrange("p (c i t) -> p c t i", i=4, t=PACK)
             engine(dst, raw[:, :, at : at + w].rearrange("p t (c i) -> p c t i", i=4))
 
+        grouped = [keep.tile([P, T * PACK], BF16, name=f"grouped{a}", align_bytes=64) for a in range(PASSES)]
+
+        def cast_chunk(a, x0, x1):
+            w = x1 - x0
+            if a == 0:
+                s = SCALAR_SHARE[w]
+                cast(nc.scalar.copy, grouped[a], raws[a, x0], x0, 0, s)
+                cast(nc.vector.tensor_copy, grouped[a], raws[a, x0], x0, s, w - s)
+            else:
+                cast(nc.scalar.copy, grouped[a], raws[a, x0], x0, 0, w)
+
         def quantise(a):
-            grouped = keep.tile([P, T * PACK], BF16, name=f"grouped{a}", align_bytes=64)
+            done = 0
             for lo, hi in QCHUNKS[a]:
                 for x0, x1 in XCHUNKS[a]:
-                    if lo <= x0 < hi:
-                        w = x1 - x0
-                        if a == 0:
-                            cast(nc.scalar.copy, grouped, raws[a, x0], x0, 0, w // 2)
-                            cast(nc.vector.tensor_copy, grouped, raws[a, x0], x0, w // 2, w // 2)
-                        else:
-                            cast(nc.scalar.copy, grouped, raws[a, x0], x0, 0, w)
+                    if done <= x0 < hi:
+                        cast_chunk(a, x0, x1)
+                        done = x1
                 nc.vector.quantize_mx(
                     out=tok_words[a][:, lo:hi].bitcast(FP8X4),
                     scales=tok_scales[4 * a : P, lo:hi],
-                    in_=grouped[:, lo * PACK : hi * PACK],
+                    in_=grouped[a][:, lo * PACK : hi * PACK],
                 )
 
         def gather_words(a, lo, hi):
             nc.vector.tensor_copy(slot_words[a][:, lo:hi], tok_words[a][:].bitcast(U32).indirect(offs_t[:, lo // 16 : hi // 16]))
 
-        ps = [psum.tile([P, C], F32, name=f"ps{e}") for e in range(E)]
+        banks = {}
 
-        def multiply(a, e):
+        def multiply(a, unit):
+            e, lo, hi = unit
+            if a == 0:
+                banks[lo] = psum.tile([P, hi - lo], F32, name=f"ps{e}")
             nc.tensor.matmul_mx(
-                out=ps[e][:],
+                out=banks[lo][:],
                 lhsT=w_t[:, e, a, :].bitcast(FP8X4),
                 lhsT_scale=ws_t[:, e * PASSES + a, :],
-                rhs=slot_words[a][:, e * C : (e + 1) * C].bitcast(FP8X4),
-                rhs_scale=slot_scales[4 * a : P, e * C : (e + 1) * C],
+                rhs=slot_words[a][:, lo:hi].bitcast(FP8X4),
+                rhs_scale=slot_scales[4 * a : P, lo:hi],
                 start=(a == 0),
                 stop=(a == PASSES - 1),
             )
+
+        def finish(unit):
+            e, lo, hi = unit
+            if unit == UNITS[-1]:
+                nc.vector.tensor_scalar(y[:, lo:hi], banks[lo][:], b_t[:, e : e + 1], 0.0, ADD, MAX)
+            else:
+                nc.scalar.activation(y[:, lo:hi], banks[lo][:], RELU, bias=b_t[:, e : e + 1])
 
         for a in range(PASSES):
             quantise(a)
@@ -134,17 +153,15 @@ def tile_routed_moe_kernel(tc, xT, w_words, w_scales, b, gate, offs, pos1, pos2,
         for lo, hi in BCHUNKS:
             nc.vector.tensor_copy(slot_scales[:, lo:hi], tok_scales[:].indirect(offs_t[:, lo // 16 : hi // 16]))
             for a in range(PASSES - 1):
-                for e in range(lo // C, hi // C):
-                    multiply(a, e)
+                for unit in UNITS:
+                    if lo < unit[2] <= hi:
+                        multiply(a, unit)
         for lo, hi in GCHUNKS:
             gather_words(PASSES - 1, lo, hi)
-            for e in range(lo // C, hi // C):
-                multiply(PASSES - 1, e)
-                cols = slice(e * C, (e + 1) * C)
-                if e == E - 1:
-                    nc.vector.tensor_scalar(y[:, cols], ps[e][:], b_t[:, e : e + 1], 0.0, ADD, MAX)
-                else:
-                    nc.scalar.activation(y[:, cols], ps[e][:], RELU, bias=b_t[:, e : e + 1])
+            for unit in UNITS:
+                if lo < unit[2] <= hi:
+                    multiply(PASSES - 1, unit)
+                    finish(unit)
 
         nc.vector.tensor_tensor(first[:], y[:].indirect(pos1_t[:]), gate_t[:, 0, :], MULT)
         pend = []

@@ -30,9 +30,8 @@ XCHUNKS = [
 ]
 QCHUNKS = [[(0, 512), (512, 768), (768, 896), (896, 1024)], XCHUNKS[2], XCHUNKS[2], XCHUNKS[2]]
 SCALAR_SHARE = {512: 192, 384: 144, 128: 48}
-GCHUNKS = [(0, 1024), (1024, 1792), (1792, 2048)]
+LCHUNKS = [(0, 768), (768, 1536), (1536, 2048)]
 WIDE = [(0, 1024), (1024, 2048)]
-BCHUNKS = [(0, 512), (512, 1280), (1280, 2048)]
 OCHUNKS = [(0, 512), (512, 896), (896, 1024)]
 UNITS = [(e, e * C, (e + 1) * C) for e in range(E)]
 
@@ -47,7 +46,7 @@ def tile_routed_moe_kernel(tc, xT, w_words, w_scales, b, gate, offs, pos1, pos2,
         pos1_t = keep.tile([P, T // 16], U16, name="pos1_t")
         pos2_t = keep.tile([P, T // 16], U16, name="pos2_t")
         tok_scales = keep.tile([P, T], U8, name="tok_scales", align_bytes=64)
-        tok_words = [keep.tile([P, 2 * T], I32, name=f"tok_words{a}", align_bytes=64) for a in range(PASSES)]
+        tok_words = [keep.tile([P, 2 * T if a < PASSES - 1 else T], I32, name=f"tok_words{a}", align_bytes=64) for a in range(PASSES)]
         slot_words = [keep.tile([P, S], U32, name=f"slot_words{a}", align_bytes=64) for a in range(PASSES)]
         slot_scales = keep.tile([P, S], U8, name="slot_scales", align_bytes=64)
         w_t = keep.tile([P, E, PASSES, N], U32, name="w_t", align_bytes=64)
@@ -63,7 +62,7 @@ def tile_routed_moe_kernel(tc, xT, w_words, w_scales, b, gate, offs, pos1, pos2,
         nc.gpsimd.memset(ws_t[:].rearrange("p g n -> p (g n)").bitcast(I32), 0)
         nc.vector.memset(warm[:], 0.0)
         nc.scalar.activation(warm[:], warm[:], RELU)
-        for a in range(PASSES):
+        for a in range(PASSES - 1):
             nc.vector.memset(tok_words[a][:, T:], 0)
 
         xv = xT.rearrange("(a p t) n -> a p t n", p=P, t=PACK)
@@ -150,18 +149,15 @@ def tile_routed_moe_kernel(tc, xT, w_words, w_scales, b, gate, offs, pos1, pos2,
             if a < PASSES - 1:
                 for lo, hi in WIDE:
                     gather_words(a, lo, hi)
-        for lo, hi in BCHUNKS:
+        for lo, hi in LCHUNKS:
             nc.vector.tensor_copy(slot_scales[:, lo:hi], tok_scales[:].indirect(offs_t[:, lo // 16 : hi // 16]))
-            for a in range(PASSES - 1):
-                for unit in UNITS:
-                    if lo < unit[2] <= hi:
-                        multiply(a, unit)
-        for lo, hi in GCHUNKS:
             gather_words(PASSES - 1, lo, hi)
-            for unit in UNITS:
-                if lo < unit[2] <= hi:
-                    multiply(PASSES - 1, unit)
-                    finish(unit)
+            units = [unit for unit in UNITS if lo < unit[2] <= hi]
+            for a in range(PASSES):
+                for unit in units:
+                    multiply(a, unit)
+            for unit in units:
+                finish(unit)
 
         nc.vector.tensor_tensor(first[:], y[:].indirect(pos1_t[:]), gate_t[:, 0, :], MULT)
         pend = []

@@ -24,11 +24,11 @@ FLOPS = 2 * S * K * N
 
 XCHUNKS = [
     [(0, 512), (512, 896), (896, 1024)],
+    [(0, 256), (256, 512), (512, 768), (768, 1024)],
     [(0, 384), (384, 768), (768, 1024)],
     [(0, 512), (512, 1024)],
-    [(0, 512), (512, 1024)],
 ]
-QCHUNKS = [[(0, 512), (512, 768), (768, 896), (896, 1024)], XCHUNKS[2], XCHUNKS[2], XCHUNKS[2]]
+QCHUNKS = [[(0, 512), (512, 768), (768, 896), (896, 1024)], XCHUNKS[3], XCHUNKS[3], XCHUNKS[3]]
 SCALAR_SHARE = {512: 192, 384: 144, 128: 48}
 LCHUNKS = [(0, 768), (768, 1536), (1536, 2048)]
 WIDE = [(0, 1024), (1024, 2048)]

from contextlib import ExitStack

import concourse.mybir as mybir

K, T, E, C, N = 2048, 1024, 8, 256, 128
P = 128
PACK = 4
PASSES = K // (P * PACK)
S = E * C

F32 = mybir.dt.float32
BF16 = mybir.dt.bfloat16
U32 = mybir.dt.uint32
I32 = mybir.dt.int32
U16 = mybir.dt.uint16
U8 = mybir.dt.uint8
FP8X4 = mybir.dt.float8_e4m3fn_x4
RELU = mybir.ActivationFunctionType.Relu
MULT = mybir.AluOpType.mult
ADD = mybir.AluOpType.add
MAX = mybir.AluOpType.max

FLOPS = 2 * S * K * N

XCHUNKS = [
    [(0, 512), (512, 896), (896, 1024)],
    [(0, 256), (256, 512), (512, 768), (768, 1024)],
    [(0, 384), (384, 768), (768, 1024)],
    [(0, 512), (512, 1024)],
]
QCHUNKS = [[(0, 512), (512, 768), (768, 896), (896, 1024)], XCHUNKS[3], XCHUNKS[3], XCHUNKS[3]]
SCALAR_SHARE = {512: 192, 384: 144, 128: 48}
LCHUNKS = [(0, 768), (768, 1536), (1536, 2048)]
WIDE = [(0, 1024), (1024, 2048)]
OCHUNKS = [(0, 512), (512, 896), (896, 1024)]
UNITS = [(e, e * C, (e + 1) * C) for e in range(E)]


def tile_routed_moe_kernel(tc, xT, w_words, w_scales, b, gate, offs, pos1, pos2, out):
    nc = tc.nc
    with ExitStack() as ctx:
        keep = ctx.enter_context(tc.tile_pool(name="keep", bufs=1))
        psum = ctx.enter_context(tc.psum_pool(name="psum", bufs=1))

        offs_t = keep.tile([P, S // 16], U16, name="offs_t")
        pos1_t = keep.tile([P, T // 16], U16, name="pos1_t")
        pos2_t = keep.tile([P, T // 16], U16, name="pos2_t")
        tok_scales = keep.tile([P, T], U8, name="tok_scales", align_bytes=64)
        tok_words = [keep.tile([P, 2 * T if a < PASSES - 1 else T], I32, name=f"tok_words{a}", align_bytes=64) for a in range(PASSES)]
        slot_words = [keep.tile([P, S], U32, name=f"slot_words{a}", align_bytes=64) for a in range(PASSES)]
        slot_scales = keep.tile([P, S], U8, name="slot_scales", align_bytes=64)
        w_t = keep.tile([P, E, PASSES, N], U32, name="w_t", align_bytes=64)
        ws_t = keep.tile([P, E * PASSES, N], U8, name="ws_t", align_bytes=64)
        b_t = keep.tile([P, E], F32, name="b_t")
        gate_t = keep.tile([P, 2, T], F32, name="gate_t")
        y = keep.tile([P, S], F32, name="y")
        first = keep.tile([P, T], F32, name="first")
        second = keep.tile([P, T], F32, name="second")
        warm = keep.tile([P, 1], F32, name="warm")

        nc.gpsimd.memset(tok_scales[:], 0)
        nc.gpsimd.memset(ws_t[:].rearrange("p g n -> p (g n)").bitcast(I32), 0)
        nc.vector.memset(warm[:], 0.0)
        nc.scalar.activation(warm[:], warm[:], RELU)
        for a in range(PASSES - 1):
            nc.vector.memset(tok_words[a][:, T:], 0)

        xv = xT.rearrange("(a p t) n -> a p t n", p=P, t=PACK)
        raws = {}
        for a in range(PASSES):
            for lo, hi in XCHUNKS[a]:
                raw = keep.tile([P, PACK, hi - lo], F32, name=f"raw{a}_{lo}")
                nc.sync.dma_start(out=raw[:], in_=xv[a, :, :, lo:hi])
                raws[a, lo] = raw
            if a == 0:
                nc.sync.dma_start(offs_t[:], offs)
        for q in range(4):
            nc.sync.dma_start(
                out=ws_t[32 * q : 32 * q + 4, :, :].rearrange("r g n -> r (g n)").bitcast(I32).rearrange("r (g n) -> r g n", g=E * PASSES),
                in_=w_scales.bitcast(I32).rearrange("e a r n -> r (e a) n")[4 * q : 4 * q + 4],
            )
        wv = w_words.rearrange("e a p n r -> p (e a) (n r)").bitcast(I32)
        wt = w_t[:].rearrange("p e a n -> p (e a) n").bitcast(I32)
        half = E * PASSES // 4
        for h in range(4):
            nc.sync.dma_start(out=wt[:, h * half : (h + 1) * half, :], in_=wv[:, h * half : (h + 1) * half, :])
        nc.sync.dma_start(b_t[:], b)
        nc.sync.dma_start(pos1_t[:], pos1)
        nc.sync.dma_start(pos2_t[:], pos2)
        for r in range(2):
            nc.sync.dma_start(gate_t[:, r, :], gate[r])

        def cast(engine, grouped, raw, lo, at, w):
            dst = grouped[:, (lo + at) * PACK : (lo + at + w) * PACK].rearrange("p (c i t) -> p c t i", i=4, t=PACK)
            engine(dst, raw[:, :, at : at + w].rearrange("p t (c i) -> p c t i", i=4))

        grouped = [keep.tile([P, T * PACK], BF16, name=f"grouped{a}", align_bytes=64) for a in range(PASSES)]

        def cast_chunk(a, x0, x1):
            w = x1 - x0
            if a == 0:
                s = SCALAR_SHARE[w]
                cast(nc.scalar.copy, grouped[a], raws[a, x0], x0, 0, s)
                cast(nc.vector.tensor_copy, grouped[a], raws[a, x0], x0, s, w - s)
            else:
                cast(nc.scalar.copy, grouped[a], raws[a, x0], x0, 0, w)

        def quantise(a):
            done = 0
            for lo, hi in QCHUNKS[a]:
                for x0, x1 in XCHUNKS[a]:
                    if done <= x0 < hi:
                        cast_chunk(a, x0, x1)
                        done = x1
                nc.vector.quantize_mx(
                    out=tok_words[a][:, lo:hi].bitcast(FP8X4),
                    scales=tok_scales[4 * a : P, lo:hi],
                    in_=grouped[a][:, lo * PACK : hi * PACK],
                )

        def gather_words(a, lo, hi):
            nc.vector.tensor_copy(slot_words[a][:, lo:hi], tok_words[a][:].bitcast(U32).indirect(offs_t[:, lo // 16 : hi // 16]))

        banks = {}

        def multiply(a, unit):
            e, lo, hi = unit
            if a == 0:
                banks[lo] = psum.tile([P, hi - lo], F32, name=f"ps{e}")
            nc.tensor.matmul_mx(
                out=banks[lo][:],
                lhsT=w_t[:, e, a, :].bitcast(FP8X4),
                lhsT_scale=ws_t[:, e * PASSES + a, :],
                rhs=slot_words[a][:, lo:hi].bitcast(FP8X4),
                rhs_scale=slot_scales[4 * a : P, lo:hi],
                start=(a == 0),
                stop=(a == PASSES - 1),
            )

        def finish(unit):
            e, lo, hi = unit
            if unit == UNITS[-1]:
                nc.vector.tensor_scalar(y[:, lo:hi], banks[lo][:], b_t[:, e : e + 1], 0.0, ADD, MAX)
            else:
                nc.scalar.activation(y[:, lo:hi], banks[lo][:], RELU, bias=b_t[:, e : e + 1])

        for a in range(PASSES):
            quantise(a)
            if a < PASSES - 1:
                for lo, hi in WIDE:
                    gather_words(a, lo, hi)
        for lo, hi in LCHUNKS:
            nc.vector.tensor_copy(slot_scales[:, lo:hi], tok_scales[:].indirect(offs_t[:, lo // 16 : hi // 16]))
            gather_words(PASSES - 1, lo, hi)
            units = [unit for unit in UNITS if lo < unit[2] <= hi]
            for a in range(PASSES):
                for unit in units:
                    multiply(a, unit)
            for unit in units:
                finish(unit)

        nc.vector.tensor_tensor(first[:], y[:].indirect(pos1_t[:]), gate_t[:, 0, :], MULT)
        pend = []
        for lo, hi in OCHUNKS:
            nc.vector.tensor_tensor(second[:, lo:hi], y[:].indirect(pos2_t[:, lo // 16 : hi // 16]), gate_t[:, 1, lo:hi], MULT)
            pend.append((lo, hi))
            if len(pend) > 1:
                combine(nc, keep, first, second, out, *pend.pop(0))
        combine(nc, keep, first, second, out, *pend.pop(0))


def combine(nc, keep, first, second, out, lo, hi):
    res = keep.tile([P, hi - lo], F32, name=f"res{lo}")
    nc.vector.tensor_tensor(res[:], first[:, lo:hi], second[:, lo:hi], ADD)
    nc.sync.dma_start(out[:, lo:hi], res[:])
